import numpy as np
import ml_dtypes


def mxq(x, axis, fmt="e4m3"):
    dtype, down = {"e4m3": (ml_dtypes.float8_e4m3fn, 7), "e5m2": (ml_dtypes.float8_e5m2, 14)}[fmt]
    v = np.moveaxis(np.asarray(x, np.float32).astype(ml_dtypes.bfloat16).astype(np.float64), axis, -1)
    blocks = v.reshape(v.shape[:-1] + (-1, 32))
    amax = np.abs(blocks).max(-1, keepdims=True)
    byte = np.maximum(np.where(amax > 0, np.frexp(amax)[1] - 1 + 127, 0) - down, 1)
    scale = np.exp2(byte - 127.0)
    codes = (blocks / scale).astype(np.float32).astype(dtype).astype(np.float64)
    return np.moveaxis((codes * scale).reshape(v.shape), -1, axis)


WIDE = False


def mx_kscale(k):
    if not WIDE:
        return np.ones(k)
    levels = np.array([10, -10, 5, -5, 0])
    if k % 512:
        return np.exp2(np.random.permutation(np.resize(levels, k // 32))).repeat(32)
    a = np.empty((k // 512, 16))
    for p in range(k // 512):
        a[p, :8] = np.random.permutation(np.resize(levels, 8))
        for g in range(8):
            far = levels[np.abs(levels - a[p, g]) >= 10]
            a[p, g + 8] = far[np.random.randint(len(far))]
    return np.exp2(a.ravel()).repeat(32)


def f64(x):
    return np.asarray(x).astype(np.float64)


def striped(idx):
    return np.tile(idx.reshape(-1, 16).T, (8, 1)).astype(np.uint16)


def unstriped(offs):
    return offs[:16].T.reshape(-1).astype(np.int64)


def pack_weight(w):
    k, n = w.shape
    w = f64(np.asarray(w, np.float32).astype(ml_dtypes.bfloat16)).reshape(k // 32, 32, n)
    amax = np.abs(w).max(1)
    byte = np.clip(np.where(amax > 0, np.frexp(amax)[1] - 1 + 127 - 7, 1), 1, 254)
    scaled = (w * np.exp2(127.0 - byte)[:, None, :]).reshape(k, n).astype(np.float32)
    words = np.ascontiguousarray(scaled.reshape(k // 512, 128, 4, n).transpose(0, 1, 3, 2)).astype(ml_dtypes.float8_e4m3fn).view(np.uint8)
    return words, np.ascontiguousarray(byte.astype(np.uint8).reshape(k // 512, 16, n))


def unpack_weight(words, scales):
    g, p, n, _ = words.shape
    vals = np.ascontiguousarray(words).view(ml_dtypes.float8_e4m3fn).astype(np.float64) * np.repeat(np.exp2(scales.astype(np.float64) - 127.0), 8, axis=1)[..., None]
    return vals.transpose(0, 1, 3, 2).reshape(g * 512, n)


K, T, S, V, N = 512, 1024, 512, 256, 128
P = 2 ** 7


def setup_inputs():
    n = np.random.standard_normal
    s = mx_kscale(K)[:, None]
    packed_xT = pack_weight(n((K, T)) * s)
    return {
        "x_words": packed_xT[0],
        "x_scales": packed_xT[1],
        "w1": (n((K, N)) / np.sqrt(K) / s).astype(np.float32),
        "fx": np.tile(np.random.uniform(0.05, 0.95, V), (P, 1)).astype(np.float32),
        "fy": np.tile(np.random.uniform(0.05, 0.95, V), (P, 1)).astype(np.float32),
        "offs": striped(np.random.permutation(T)[:S]),
        "c00": striped(np.random.permutation(S)[:V]),
        "c01": striped(np.random.permutation(S)[:V]),
        "c10": striped(np.random.permutation(S)[:V]),
        "c11": striped(np.random.permutation(S)[:V]),
    }


def reference(x_words, x_scales, w1, fx, fy, offs, c00, c01, c10, c11):
    xq = unpack_weight(x_words, x_scales)[:, unstriped(offs)]
    y = mxq(f64(w1), 0, "e4m3").T @ xq
    top = y[:, unstriped(c00)] + (y[:, unstriped(c01)] - y[:, unstriped(c00)]) * f64(fx)[:1]
    low = y[:, unstriped(c10)] + (y[:, unstriped(c11)] - y[:, unstriped(c10)]) * f64(fx)[:1]
    return top + (low - top) * f64(fy)[:1]

@@ -1,0 +1,110 @@
+from contextlib import ExitStack
+
+import concourse.mybir as mybir
+
+K, T, S, V, N = 512, 1024, 512, 256, 128
+FLOPS = 2 * K * S * N
+
+F32 = mybir.dt.float32
+BF16 = mybir.dt.bfloat16
+I32 = mybir.dt.int32
+U32 = mybir.dt.uint32
+U16 = mybir.dt.uint16
+U8 = mybir.dt.uint8
+FP8X4 = mybir.dt.float8_e4m3fn_x4
+ALU = mybir.AluOpType
+
+P = 128
+
+
+def tile_picked_bilin_none_p_kernel(tc, x_words, x_scales, w1, fx, fy, offs, c00, c01, c10, c11, out):
+    nc = tc.nc
+    with ExitStack() as ctx:
+        keep = ctx.enter_context(tc.tile_pool(name="keep", bufs=1))
+        psum = ctx.enter_context(tc.psum_pool(name="psum", bufs=1))
+
+        scale_win = keep.tile([P, T], U8, align_bytes=64)
+        nc.vector.memset(scale_win[:].bitcast(I32), 0)
+        offs_sb = keep.tile([P, S // 16], U16)
+        word_win = keep.tile([P, T], U32, align_bytes=64)
+        w_raw = keep.tile([P, 4, N], F32, align_bytes=64, tag="raw")
+        fx_sb = keep.tile([P, V], F32, align_bytes=64)
+        fy_sb = keep.tile([P, V], F32, align_bytes=64)
+        l11 = keep.tile([P, V // 16], U16)
+        l10 = keep.tile([P, V // 16], U16)
+        l01 = keep.tile([P, V // 16], U16)
+        l00 = keep.tile([P, V // 16], U16)
+
+        def load_scales(eng, q):
+            eng.dma_start(scale_win[32 * q : 32 * q + 4, :].bitcast(I32), x_scales[0, 4 * q : 4 * q + 4, :].bitcast(I32))
+
+        load_scales(nc.sync, 0)
+        load_scales(nc.sync, 1)
+        load_scales(nc.scalar, 2)
+        load_scales(nc.scalar, 3)
+        nc.sync.dma_start(offs_sb[:], offs)
+        nc.sync.dma_start(w_raw[:], w1.rearrange("(p j) m -> p j m", j=4))
+        nc.sync.dma_start(l11[:], c11)
+        nc.sync.dma_start(word_win[:].bitcast(I32), x_words[0].rearrange("p c r -> p (c r)").bitcast(I32))
+        nc.sync.dma_start(fx_sb[:], fx)
+        nc.sync.dma_start(fy_sb[:], fy)
+        nc.sync.dma_start(l10[:], c10)
+        nc.sync.dma_start(l01[:], c01)
+        nc.sync.dma_start(l00[:], c00)
+
+        w_bf = keep.tile([P, N, 4], BF16, align_bytes=64)
+        nc.scalar.copy(w_bf[:].rearrange("p (c i) t -> p c t i", i=4), w_raw[:].rearrange("p t (c i) -> p c t i", i=4))
+
+        x_sc = keep.tile([P, S], U8, align_bytes=64)
+        w_codes = keep.tile([P, N], U32, align_bytes=64)
+        w_sc = keep.tile([P, N], U8, align_bytes=64)
+        xa = keep.tile([P, 256], U32, align_bytes=64, tag="shared")
+        y = keep.tile([P, S], F32, align_bytes=64)
+
+        def gather_scales(a, b):
+            nc.vector.tensor_copy(x_sc[:, a:b], scale_win[:].indirect(offs_sb[:, a // 16 : b // 16]))
+
+        def gather_words(xc, o, a, b):
+            nc.vector.tensor_copy(xc[:, a - o : b - o], word_win[:].indirect(offs_sb[:, a // 16 : b // 16]))
+
+        def quantize():
+            nc.vector.quantize_mx(out=w_codes[:].bitcast(FP8X4), scales=w_sc[:], in_=w_bf[:].rearrange("p m t -> p (m t)"))
+
+        def project(xc, o, a, b):
+            acc = psum.tile([P, 512], F32, name="acc%d" % a)
+            nc.tensor.matmul_mx(out=acc[:, 0 : b - a], lhsT=w_codes[:].bitcast(FP8X4), lhsT_scale=w_sc[:],
+                                rhs=xc[:, a - o : b - o].bitcast(FP8X4), rhs_scale=x_sc[:, a:b], start=True, stop=True)
+            nc.scalar.copy(y[:, a:b], acc[:, 0 : b - a])
+
+        gather_scales(0, 512)
+        gather_words(xa, 0, 0, 256)
+        quantize()
+        project(xa, 0, 0, 256)
+        xb = keep.tile([P, 256], U32, align_bytes=64, tag="raw")
+        gather_words(xb, 256, 256, 384)
+        project(xb, 256, 256, 384)
+        gather_words(xb, 256, 384, 512)
+        project(xb, 256, 384, 512)
+
+        wts = keep.tile([P, 4, V], F32, align_bytes=64, tag="shared")
+        w11, n10, n01, n00 = wts[:, 0, :], wts[:, 1, :], wts[:, 2, :], wts[:, 3, :]
+        nc.vector.scalar_tensor_tensor(n10, fx_sb[:], 1.0, fy_sb[:], ALU.subtract, ALU.mult)
+        nc.vector.tensor_tensor(w11, fx_sb[:], fy_sb[:], ALU.mult)
+        nc.vector.scalar_tensor_tensor(n01, fy_sb[:], 1.0, fx_sb[:], ALU.subtract, ALU.mult)
+        nc.vector.scalar_tensor_tensor(n00, fx_sb[:], 1.0, n10, ALU.subtract, ALU.subtract)
+
+        g11 = keep.tile([P, V], F32)
+        g10 = keep.tile([P, V], F32)
+        g01 = keep.tile([P, V], F32)
+        g00 = keep.tile([P, V], F32)
+        s1 = keep.tile([P, V], F32)
+        s2 = keep.tile([P, V], F32)
+        res = keep.tile([P, V], F32)
+        nc.vector.tensor_tensor(g11[:], y[:].indirect(l11[:]), w11, ALU.mult)
+        nc.vector.tensor_tensor(g10[:], y[:].indirect(l10[:]), n10, ALU.mult)
+        nc.vector.tensor_tensor(g01[:], y[:].indirect(l01[:]), n01, ALU.mult)
+        nc.vector.tensor_tensor(s1[:], g11[:], g10[:], ALU.subtract)
+        nc.vector.tensor_tensor(g00[:], y[:].indirect(l00[:]), n00, ALU.mult)
+        nc.vector.tensor_tensor(s2[:], s1[:], g01[:], ALU.subtract)
+        nc.vector.tensor_tensor(res[:], s2[:], g00[:], ALU.subtract)
+        nc.sync.dma_start(out, res[:])

@@ -21,13 +21,14 @@ def tile_picked_bilin_none_p_kernel(tc, x_words, x_scales, w1, fx, fy, offs, c00
     nc = tc.nc
     with ExitStack() as ctx:
         keep = ctx.enter_context(tc.tile_pool(name="keep", bufs=1))
+        reuse = ctx.enter_context(tc.tile_pool(name="reuse", bufs=1))
         psum = ctx.enter_context(tc.psum_pool(name="psum", bufs=1))
 
         scale_win = keep.tile([P, T], U8, align_bytes=64)
         nc.vector.memset(scale_win[:].bitcast(I32), 0)
         offs_sb = keep.tile([P, S // 16], U16)
         word_win = keep.tile([P, T], U32, align_bytes=64)
-        w_raw = keep.tile([P, 4, N], F32, align_bytes=64, tag="raw")
+        w_raw = reuse.tile([P, 4, N], F32, align_bytes=64, offset=3072)
         fx_sb = keep.tile([P, V], F32, align_bytes=64)
         fy_sb = keep.tile([P, V], F32, align_bytes=64)
         l11 = keep.tile([P, V // 16], U16)
@@ -40,8 +41,8 @@ def tile_picked_bilin_none_p_kernel(tc, x_words, x_scales, w1, fx, fy, offs, c00
 
         load_scales(nc.sync, 0)
         load_scales(nc.sync, 1)
-        load_scales(nc.scalar, 2)
-        load_scales(nc.scalar, 3)
+        load_scales(nc.sync, 2)
+        load_scales(nc.sync, 3)
         nc.sync.dma_start(offs_sb[:], offs)
         nc.sync.dma_start(w_raw[:], w1.rearrange("(p j) m -> p j m", j=4))
         nc.sync.dma_start(l11[:], c11)
@@ -58,7 +59,7 @@ def tile_picked_bilin_none_p_kernel(tc, x_words, x_scales, w1, fx, fy, offs, c00
         x_sc = keep.tile([P, S], U8, align_bytes=64)
         w_codes = keep.tile([P, N], U32, align_bytes=64)
         w_sc = keep.tile([P, N], U8, align_bytes=64)
-        xa = keep.tile([P, 256], U32, align_bytes=64, tag="shared")
+        xa = keep.tile([P, 256], U32, align_bytes=64)
         y = keep.tile([P, S], F32, align_bytes=64)
 
         def gather_scales(a, b):
@@ -80,13 +81,13 @@ def tile_picked_bilin_none_p_kernel(tc, x_words, x_scales, w1, fx, fy, offs, c00
         gather_words(xa, 0, 0, 256)
         quantize()
         project(xa, 0, 0, 256)
-        xb = keep.tile([P, 256], U32, align_bytes=64, tag="raw")
+        xb = reuse.tile([P, 256], U32, align_bytes=64, offset=4096)
         gather_words(xb, 256, 256, 384)
         project(xb, 256, 256, 384)
         gather_words(xb, 256, 384, 512)
         project(xb, 256, 384, 512)
 
-        wts = keep.tile([P, 4, V], F32, align_bytes=64, tag="shared")
+        wts = reuse.tile([P, 4, V], F32, align_bytes=64, offset=0)
         w11, n10, n01, n00 = wts[:, 0, :], wts[:, 1, :], wts[:, 2, :], wts[:, 3, :]
         nc.vector.scalar_tensor_tensor(n10, fx_sb[:], 1.0, fy_sb[:], ALU.subtract, ALU.mult)
         nc.vector.tensor_tensor(w11, fx_sb[:], fy_sb[:], ALU.mult)

@@ -41,8 +41,8 @@ def tile_picked_bilin_none_p_kernel(tc, x_words, x_scales, w1, fx, fy, offs, c00
 
         load_scales(nc.sync, 0)
         load_scales(nc.sync, 1)
-        load_scales(nc.sync, 2)
-        load_scales(nc.sync, 3)
+        load_scales(nc.scalar, 2)
+        load_scales(nc.scalar, 3)
         nc.sync.dma_start(offs_sb[:], offs)
         nc.sync.dma_start(w_raw[:], w1.rearrange("(p j) m -> p j m", j=4))
         nc.sync.dma_start(l11[:], c11)
@@ -54,7 +54,7 @@ def tile_picked_bilin_none_p_kernel(tc, x_words, x_scales, w1, fx, fy, offs, c00
         nc.sync.dma_start(l00[:], c00)
 
         w_bf = keep.tile([P, N, 4], BF16, align_bytes=64)
-        nc.scalar.copy(w_bf[:].rearrange("p (c i) t -> p c t i", i=4), w_raw[:].rearrange("p t (c i) -> p c t i", i=4))
+        nc.scalar.copy(w_bf[:], w_raw[:].rearrange("p t m -> p m t"))
 
         x_sc = keep.tile([P, S], U8, align_bytes=64)
         w_codes = keep.tile([P, N], U32, align_bytes=64)

@@ -13,6 +13,7 @@ U16 = mybir.dt.uint16
 U8 = mybir.dt.uint8
 FP8X4 = mybir.dt.float8_e4m3fn_x4
 ALU = mybir.AluOpType
+COPY = mybir.ActivationFunctionType.Copy
 
 P = 128
 
@@ -29,7 +30,7 @@ def tile_picked_bilin_none_p_kernel(tc, x_words, x_scales, w1, fx, fy, offs, c00
         offs_sb = keep.tile([P, S // 16], U16)
         word_win = keep.tile([P, T], U32, align_bytes=64)
         w_raw = reuse.tile([P, 4, N], F32, align_bytes=64, offset=3072)
-        fx_sb = keep.tile([P, V], F32, align_bytes=64)
+        along_x = keep.tile([P, 2, V], F32, align_bytes=64)
         fy_sb = keep.tile([P, V], F32, align_bytes=64)
         l11 = keep.tile([P, V // 16], U16)
         l10 = keep.tile([P, V // 16], U16)
@@ -45,16 +46,18 @@ def tile_picked_bilin_none_p_kernel(tc, x_words, x_scales, w1, fx, fy, offs, c00
         load_scales(nc.scalar, 3)
         nc.sync.dma_start(offs_sb[:], offs)
         nc.sync.dma_start(w_raw[:], w1.rearrange("(p j) m -> p j m", j=4))
-        nc.sync.dma_start(l11[:], c11)
         nc.sync.dma_start(word_win[:].bitcast(I32), x_words[0].rearrange("p c r -> p (c r)").bitcast(I32))
-        nc.sync.dma_start(fx_sb[:], fx)
+        nc.sync.dma_start(along_x[:, 1, :], fx)
         nc.sync.dma_start(fy_sb[:], fy)
+        nc.sync.dma_start(l11[:], c11)
         nc.sync.dma_start(l10[:], c10)
         nc.sync.dma_start(l01[:], c01)
         nc.sync.dma_start(l00[:], c00)
 
         w_bf = keep.tile([P, N, 4], BF16, align_bytes=64)
         nc.scalar.copy(w_bf[:], w_raw[:].rearrange("p t m -> p m t"))
+
+        nc.scalar.activation(along_x[:, 0, :], along_x[:, 1, :], COPY, bias=1.0, scale=-1.0)
 
         x_sc = keep.tile([P, S], U8, align_bytes=64)
         w_codes = keep.tile([P, N], U32, align_bytes=64)
@@ -87,25 +90,28 @@ def tile_picked_bilin_none_p_kernel(tc, x_words, x_scales, w1, fx, fy, offs, c00
         gather_words(xb, 256, 384, 512)
         project(xb, 256, 384, 512)
 
-        wts = reuse.tile([P, 4, V], F32, align_bytes=64, offset=0)
-        w11, n10, n01, n00 = wts[:, 0, :], wts[:, 1, :], wts[:, 2, :], wts[:, 3, :]
-        nc.vector.scalar_tensor_tensor(n10, fx_sb[:], 1.0, fy_sb[:], ALU.subtract, ALU.mult)
-        nc.vector.tensor_tensor(w11, fx_sb[:], fy_sb[:], ALU.mult)
-        nc.vector.scalar_tensor_tensor(n01, fy_sb[:], 1.0, fx_sb[:], ALU.subtract, ALU.mult)
-        nc.vector.scalar_tensor_tensor(n00, fx_sb[:], 1.0, n10, ALU.subtract, ALU.subtract)
+        wts = reuse.tile([P, 2, 2, V], F32, align_bytes=64, offset=0)
+        fy_twice = fy_sb[:].unsqueeze(1).to_broadcast([P, 2, V])
+        nc.vector.tensor_tensor(wts[:, 1, :, :], fy_twice, along_x[:], ALU.mult)
+        nc.vector.scalar_tensor_tensor(wts[:, 0, :, :], fy_twice, 1.0, along_x[:], ALU.subtract, ALU.mult)
+        w11, n10, n01, n00 = wts[:, 1, 1, :], wts[:, 1, 0, :], wts[:, 0, 1, :], wts[:, 0, 0, :]
 
         g11 = keep.tile([P, V], F32)
-        g10 = keep.tile([P, V], F32)
+        g10 = reuse.tile([P, V], F32, align_bytes=64, offset=6144)
         g01 = keep.tile([P, V], F32)
-        g00 = keep.tile([P, V], F32)
+        cut = 160
+        g00a = keep.tile([P, cut], F32)
         s1 = keep.tile([P, V], F32)
         s2 = keep.tile([P, V], F32)
         res = keep.tile([P, V], F32)
         nc.vector.tensor_tensor(g11[:], y[:].indirect(l11[:]), w11, ALU.mult)
         nc.vector.tensor_tensor(g10[:], y[:].indirect(l10[:]), n10, ALU.mult)
         nc.vector.tensor_tensor(g01[:], y[:].indirect(l01[:]), n01, ALU.mult)
-        nc.vector.tensor_tensor(s1[:], g11[:], g10[:], ALU.subtract)
-        nc.vector.tensor_tensor(g00[:], y[:].indirect(l00[:]), n00, ALU.mult)
+        nc.vector.tensor_tensor(s1[:], g11[:], g10[:], ALU.add)
+        nc.vector.tensor_tensor(g00a[:], y[:].indirect(l00[:, 0 : cut // 16]), n00[:, 0:cut], ALU.mult)
         nc.vector.tensor_tensor(s2[:], s1[:], g01[:], ALU.subtract)
-        nc.vector.tensor_tensor(res[:], s2[:], g00[:], ALU.subtract)
+        g00b = reuse.tile([P, V - cut], F32, align_bytes=64, offset=6144)
+        nc.vector.tensor_tensor(g00b[:], y[:].indirect(l00[:, cut // 16 : V // 16]), n00[:, cut:V], ALU.mult)
+        nc.vector.tensor_tensor(res[:, 0:cut], s2[:, 0:cut], g00a[:], ALU.subtract)
+        nc.vector.tensor_tensor(res[:, cut:V], s2[:, cut:V], g00b[:], ALU.subtract)
         nc.sync.dma_start(out, res[:])

@@ -62,7 +62,6 @@ def tile_picked_bilin_none_p_kernel(tc, x_words, x_scales, w1, fx, fy, offs, c00
         x_sc = keep.tile([P, S], U8, align_bytes=64)
         w_codes = keep.tile([P, N], U32, align_bytes=64)
         w_sc = keep.tile([P, N], U8, align_bytes=64)
-        xa = keep.tile([P, 256], U32, align_bytes=64)
         y = keep.tile([P, S], F32, align_bytes=64)
 
         def gather_scales(a, b):
@@ -81,14 +80,14 @@ def tile_picked_bilin_none_p_kernel(tc, x_words, x_scales, w1, fx, fy, offs, c00
             nc.scalar.copy(y[:, a:b], acc[:, 0 : b - a])
 
         gather_scales(0, 512)
-        gather_words(xa, 0, 0, 256)
         quantize()
+        xa = reuse.tile([P, S], U32, align_bytes=64, offset=4096)
+        gather_words(xa, 0, 0, 256)
         project(xa, 0, 0, 256)
-        xb = reuse.tile([P, 256], U32, align_bytes=64, offset=4096)
-        gather_words(xb, 256, 256, 384)
-        project(xb, 256, 256, 384)
-        gather_words(xb, 256, 384, 512)
-        project(xb, 256, 384, 512)
+        gather_words(xa, 0, 256, 384)
+        project(xa, 0, 256, 384)
+        gather_words(xa, 0, 384, 512)
+        project(xa, 0, 384, 512)
 
         wts = reuse.tile([P, 2, 2, V], F32, align_bytes=64, offset=0)
         fy_twice = fy_sb[:].unsqueeze(1).to_broadcast([P, 2, V])

@@ -47,10 +47,10 @@ def tile_picked_bilin_none_p_kernel(tc, x_words, x_scales, w1, fx, fy, offs, c00
         nc.sync.dma_start(offs_sb[:], offs)
         nc.sync.dma_start(w_raw[:], w1.rearrange("(p j) m -> p j m", j=4))
         nc.sync.dma_start(word_win[:].bitcast(I32), x_words[0].rearrange("p c r -> p (c r)").bitcast(I32))
-        nc.sync.dma_start(along_x[:, 1, :], fx)
-        nc.sync.dma_start(fy_sb[:], fy)
         nc.sync.dma_start(l11[:], c11)
         nc.sync.dma_start(l10[:], c10)
+        nc.sync.dma_start(along_x[:, 1, :], fx)
+        nc.sync.dma_start(fy_sb[:], fy)
         nc.sync.dma_start(l01[:], c01)
         nc.sync.dma_start(l00[:], c00)
 

@@ -38,7 +38,7 @@ def tile_picked_bilin_none_p_kernel(tc, x_words, x_scales, w1, fx, fy, offs, c00
         l00 = keep.tile([P, V // 16], U16)
 
         def load_scales(eng, q):
-            eng.dma_start(scale_win[32 * q : 32 * q + 4, :].bitcast(I32), x_scales[0, 4 * q : 4 * q + 4, :].bitcast(I32))
+            eng.dma_start(scale_win[q:P:32, :].bitcast(I32), x_scales[0].rearrange("(a r) c -> r a c", r=4)[q].bitcast(I32))
 
         load_scales(nc.sync, 0)
         load_scales(nc.sync, 1)

@@ -47,15 +47,17 @@ def tile_picked_bilin_none_p_kernel(tc, x_words, x_scales, w1, fx, fy, offs, c00
         nc.sync.dma_start(offs_sb[:], offs)
         nc.sync.dma_start(w_raw[:], w1.rearrange("(p j) m -> p j m", j=4))
         nc.sync.dma_start(word_win[:].bitcast(I32), x_words[0].rearrange("p c r -> p (c r)").bitcast(I32))
+        nc.sync.dma_start(along_x[:, 1, :], fx)
         nc.sync.dma_start(l11[:], c11)
         nc.sync.dma_start(l10[:], c10)
-        nc.sync.dma_start(along_x[:, 1, :], fx)
         nc.sync.dma_start(fy_sb[:], fy)
         nc.sync.dma_start(l01[:], c01)
         nc.sync.dma_start(l00[:], c00)
 
         w_bf = keep.tile([P, N, 4], BF16, align_bytes=64)
-        nc.scalar.copy(w_bf[:], w_raw[:].rearrange("p t m -> p m t"))
+        share = 80
+        nc.scalar.copy(w_bf[:, 0:share, :], w_raw[:, :, 0:share].rearrange("p t m -> p m t"))
+        nc.gpsimd.tensor_copy(w_bf[:, share:N, :], w_raw[:, :, share:N].rearrange("p t m -> p m t"))
 
         nc.scalar.activation(along_x[:, 0, :], along_x[:, 1, :], COPY, bias=1.0, scale=-1.0)
 

@@ -27,6 +27,9 @@ def tile_picked_bilin_none_p_kernel(tc, x_words, x_scales, w1, fx, fy, offs, c00
 
         scale_win = keep.tile([P, T], U8, align_bytes=64)
         nc.vector.memset(scale_win[:].bitcast(I32), 0)
+        warm_in = keep.tile([P, 8], F32)
+        warm_out = keep.tile([P, 8], F32)
+        nc.vector.memset(warm_in[:], 0.0)
         offs_sb = keep.tile([P, S // 16], U16)
         word_win = keep.tile([P, T], U32, align_bytes=64)
         w_raw = reuse.tile([P, 4, N], F32, align_bytes=64, offset=3072)
@@ -40,21 +43,24 @@ def tile_picked_bilin_none_p_kernel(tc, x_words, x_scales, w1, fx, fy, offs, c00
         def load_scales(eng, q):
             eng.dma_start(scale_win[q:P:32, :].bitcast(I32), x_scales[0].rearrange("(a r) c -> r a c", r=4)[q].bitcast(I32))
 
+        w_rows = w1.rearrange("(p j) m -> p j m", j=4)
+        nc.scalar.dma_start(w_raw[:, 0:2, :], w_rows[:, 0:2, :])
         load_scales(nc.sync, 0)
         load_scales(nc.sync, 1)
         load_scales(nc.scalar, 2)
         load_scales(nc.scalar, 3)
         nc.sync.dma_start(offs_sb[:], offs)
-        nc.sync.dma_start(w_raw[:], w1.rearrange("(p j) m -> p j m", j=4))
+        nc.sync.dma_start(w_raw[:, 2:4, :], w_rows[:, 2:4, :])
         nc.sync.dma_start(word_win[:].bitcast(I32), x_words[0].rearrange("p c r -> p (c r)").bitcast(I32))
         nc.sync.dma_start(along_x[:, 1, :], fx)
         nc.sync.dma_start(l11[:], c11)
         nc.sync.dma_start(l10[:], c10)
-        nc.sync.dma_start(fy_sb[:], fy)
         nc.sync.dma_start(l01[:], c01)
         nc.sync.dma_start(l00[:], c00)
+        nc.sync.dma_start(fy_sb[:], fy)
 
         w_bf = keep.tile([P, N, 4], BF16, align_bytes=64)
+        nc.scalar.copy(warm_out[:], warm_in[:])
         share = 80
         nc.scalar.copy(w_bf[:, 0:share, :], w_raw[:, :, 0:share].rearrange("p t m -> p m t"))
         nc.gpsimd.tensor_copy(w_bf[:, share:N, :], w_raw[:, :, share:N].rearrange("p t m -> p m t"))

@@ -55,9 +55,9 @@ def tile_picked_bilin_none_p_kernel(tc, x_words, x_scales, w1, fx, fy, offs, c00
         nc.sync.dma_start(along_x[:, 1, :], fx)
         nc.sync.dma_start(l11[:], c11)
         nc.sync.dma_start(l10[:], c10)
+        nc.sync.dma_start(fy_sb[:], fy)
         nc.sync.dma_start(l01[:], c01)
         nc.sync.dma_start(l00[:], c00)
-        nc.sync.dma_start(fy_sb[:], fy)
 
         w_bf = keep.tile([P, N, 4], BF16, align_bytes=64)
         nc.scalar.copy(warm_out[:], warm_in[:])

@@ -44,12 +44,12 @@ def tile_picked_bilin_none_p_kernel(tc, x_words, x_scales, w1, fx, fy, offs, c00
             eng.dma_start(scale_win[q:P:32, :].bitcast(I32), x_scales[0].rearrange("(a r) c -> r a c", r=4)[q].bitcast(I32))
 
         w_rows = w1.rearrange("(p j) m -> p j m", j=4)
-        nc.scalar.dma_start(w_raw[:, 0:2, :], w_rows[:, 0:2, :])
+        nc.sync.dma_start(offs_sb[:], offs)
+        nc.sync.dma_start(w_raw[:, 0:2, :], w_rows[:, 0:2, :])
         load_scales(nc.sync, 0)
         load_scales(nc.sync, 1)
         load_scales(nc.scalar, 2)
         load_scales(nc.scalar, 3)
-        nc.sync.dma_start(offs_sb[:], offs)
         nc.sync.dma_start(w_raw[:, 2:4, :], w_rows[:, 2:4, :])
         nc.sync.dma_start(word_win[:].bitcast(I32), x_words[0].rearrange("p c r -> p (c r)").bitcast(I32))
         nc.sync.dma_start(along_x[:, 1, :], fx)

@@ -27,12 +27,10 @@ def tile_picked_bilin_none_p_kernel(tc, x_words, x_scales, w1, fx, fy, offs, c00
 
         scale_win = keep.tile([P, T], U8, align_bytes=64)
         nc.vector.memset(scale_win[:].bitcast(I32), 0)
-        warm_in = keep.tile([P, 8], F32)
-        warm_out = keep.tile([P, 8], F32)
-        nc.vector.memset(warm_in[:], 0.0)
         offs_sb = keep.tile([P, S // 16], U16)
         word_win = keep.tile([P, T], U32, align_bytes=64)
-        w_raw = reuse.tile([P, 4, N], F32, align_bytes=64, offset=3072)
+        w_lo = keep.tile([P, 2, N], F32, align_bytes=64)
+        w_hi = reuse.tile([P, 2, N], F32, align_bytes=64, offset=3584)
         along_x = keep.tile([P, 2, V], F32, align_bytes=64)
         fy_sb = keep.tile([P, V], F32, align_bytes=64)
         l11 = keep.tile([P, V // 16], U16)
@@ -44,13 +42,13 @@ def tile_picked_bilin_none_p_kernel(tc, x_words, x_scales, w1, fx, fy, offs, c00
             eng.dma_start(scale_win[q:P:32, :].bitcast(I32), x_scales[0].rearrange("(a r) c -> r a c", r=4)[q].bitcast(I32))
 
         w_rows = w1.rearrange("(p j) m -> p j m", j=4)
+        nc.sync.dma_start(w_lo[:], w_rows[:, 0:2, :])
         nc.sync.dma_start(offs_sb[:], offs)
-        nc.sync.dma_start(w_raw[:, 0:2, :], w_rows[:, 0:2, :])
         load_scales(nc.sync, 0)
         load_scales(nc.sync, 1)
         load_scales(nc.scalar, 2)
         load_scales(nc.scalar, 3)
-        nc.sync.dma_start(w_raw[:, 2:4, :], w_rows[:, 2:4, :])
+        nc.sync.dma_start(w_hi[:], w_rows[:, 2:4, :])
         nc.sync.dma_start(word_win[:].bitcast(I32), x_words[0].rearrange("p c r -> p (c r)").bitcast(I32))
         nc.sync.dma_start(along_x[:, 1, :], fx)
         nc.sync.dma_start(l11[:], c11)
@@ -60,10 +58,10 @@ def tile_picked_bilin_none_p_kernel(tc, x_words, x_scales, w1, fx, fy, offs, c00
         nc.sync.dma_start(l00[:], c00)
 
         w_bf = keep.tile([P, N, 4], BF16, align_bytes=64)
-        nc.scalar.copy(warm_out[:], warm_in[:])
         share = 80
-        nc.scalar.copy(w_bf[:, 0:share, :], w_raw[:, :, 0:share].rearrange("p t m -> p m t"))
-        nc.gpsimd.tensor_copy(w_bf[:, share:N, :], w_raw[:, :, share:N].rearrange("p t m -> p m t"))
+        nc.scalar.copy(w_bf[:, :, 0:2], w_lo[:].rearrange("p t m -> p m t"))
+        nc.scalar.copy(w_bf[:, 0:share, 2:4], w_hi[:, :, 0:share].rearrange("p t m -> p m t"))
+        nc.gpsimd.tensor_copy(w_bf[:, share:N, 2:4], w_hi[:, :, share:N].rearrange("p t m -> p m t"))
 
         nc.scalar.activation(along_x[:, 0, :], along_x[:, 1, :], COPY, bias=1.0, scale=-1.0)
 

@@ -29,8 +29,7 @@ def tile_picked_bilin_none_p_kernel(tc, x_words, x_scales, w1, fx, fy, offs, c00
         nc.vector.memset(scale_win[:].bitcast(I32), 0)
         offs_sb = keep.tile([P, S // 16], U16)
         word_win = keep.tile([P, T], U32, align_bytes=64)
-        w_lo = keep.tile([P, 2, N], F32, align_bytes=64)
-        w_hi = reuse.tile([P, 2, N], F32, align_bytes=64, offset=3584)
+        w_raw = reuse.tile([P, 4, N], F32, align_bytes=64, offset=3072)
         along_x = keep.tile([P, 2, V], F32, align_bytes=64)
         fy_sb = keep.tile([P, V], F32, align_bytes=64)
         l11 = keep.tile([P, V // 16], U16)
@@ -42,13 +41,13 @@ def tile_picked_bilin_none_p_kernel(tc, x_words, x_scales, w1, fx, fy, offs, c00
             eng.dma_start(scale_win[q:P:32, :].bitcast(I32), x_scales[0].rearrange("(a r) c -> r a c", r=4)[q].bitcast(I32))
 
         w_rows = w1.rearrange("(p j) m -> p j m", j=4)
-        nc.sync.dma_start(w_lo[:], w_rows[:, 0:2, :])
+        nc.sync.dma_start(w_raw[:, 0:3, :], w_rows[:, 0:3, :])
         nc.sync.dma_start(offs_sb[:], offs)
         load_scales(nc.sync, 0)
         load_scales(nc.sync, 1)
         load_scales(nc.scalar, 2)
         load_scales(nc.scalar, 3)
-        nc.sync.dma_start(w_hi[:], w_rows[:, 2:4, :])
+        nc.sync.dma_start(w_raw[:, 3:4, :], w_rows[:, 3:4, :])
         nc.sync.dma_start(word_win[:].bitcast(I32), x_words[0].rearrange("p c r -> p (c r)").bitcast(I32))
         nc.sync.dma_start(along_x[:, 1, :], fx)
         nc.sync.dma_start(l11[:], c11)
@@ -59,9 +58,9 @@ def tile_picked_bilin_none_p_kernel(tc, x_words, x_scales, w1, fx, fy, offs, c00
 
         w_bf = keep.tile([P, N, 4], BF16, align_bytes=64)
         share = 80
-        nc.scalar.copy(w_bf[:, :, 0:2], w_lo[:].rearrange("p t m -> p m t"))
-        nc.scalar.copy(w_bf[:, 0:share, 2:4], w_hi[:, :, 0:share].rearrange("p t m -> p m t"))
-        nc.gpsimd.tensor_copy(w_bf[:, share:N, 2:4], w_hi[:, :, share:N].rearrange("p t m -> p m t"))
+        nc.scalar.copy(w_bf[:, :, 0:2], w_raw[:, 0:2, :].rearrange("p t m -> p m t"))
+        nc.scalar.copy(w_bf[:, 0:share, 2:4], w_raw[:, 2:4, 0:share].rearrange("p t m -> p m t"))
+        nc.gpsimd.tensor_copy(w_bf[:, share:N, 2:4], w_raw[:, 2:4, share:N].rearrange("p t m -> p m t"))
 
         nc.scalar.activation(along_x[:, 0, :], along_x[:, 1, :], COPY, bias=1.0, scale=-1.0)
 

@@ -45,7 +45,7 @@ def tile_picked_bilin_none_p_kernel(tc, x_words, x_scales, w1, fx, fy, offs, c00
         nc.sync.dma_start(offs_sb[:], offs)
         load_scales(nc.sync, 0)
         load_scales(nc.sync, 1)
-        load_scales(nc.scalar, 2)
+        load_scales(nc.sync, 2)
         load_scales(nc.scalar, 3)
         nc.sync.dma_start(w_raw[:, 3:4, :], w_rows[:, 3:4, :])
         nc.sync.dma_start(word_win[:].bitcast(I32), x_words[0].rearrange("p c r -> p (c r)").bitcast(I32))

@@ -41,13 +41,12 @@ def tile_picked_bilin_none_p_kernel(tc, x_words, x_scales, w1, fx, fy, offs, c00
             eng.dma_start(scale_win[q:P:32, :].bitcast(I32), x_scales[0].rearrange("(a r) c -> r a c", r=4)[q].bitcast(I32))
 
         w_rows = w1.rearrange("(p j) m -> p j m", j=4)
-        nc.sync.dma_start(w_raw[:, 0:3, :], w_rows[:, 0:3, :])
+        nc.sync.dma_start(w_raw[:], w_rows)
         nc.sync.dma_start(offs_sb[:], offs)
         load_scales(nc.sync, 0)
         load_scales(nc.sync, 1)
         load_scales(nc.sync, 2)
         load_scales(nc.scalar, 3)
-        nc.sync.dma_start(w_raw[:, 3:4, :], w_rows[:, 3:4, :])
         nc.sync.dma_start(word_win[:].bitcast(I32), x_words[0].rearrange("p c r -> p (c r)").bitcast(I32))
         nc.sync.dma_start(along_x[:, 1, :], fx)
         nc.sync.dma_start(l11[:], c11)
@@ -58,9 +57,8 @@ def tile_picked_bilin_none_p_kernel(tc, x_words, x_scales, w1, fx, fy, offs, c00
 
         w_bf = keep.tile([P, N, 4], BF16, align_bytes=64)
         share = 80
-        nc.scalar.copy(w_bf[:, :, 0:2], w_raw[:, 0:2, :].rearrange("p t m -> p m t"))
-        nc.scalar.copy(w_bf[:, 0:share, 2:4], w_raw[:, 2:4, 0:share].rearrange("p t m -> p m t"))
-        nc.gpsimd.tensor_copy(w_bf[:, share:N, 2:4], w_raw[:, 2:4, share:N].rearrange("p t m -> p m t"))
+        nc.scalar.copy(w_bf[:, 0:share, :], w_raw[:, :, 0:share].rearrange("p t m -> p m t"))
+        nc.gpsimd.tensor_copy(w_bf[:, share:N, :], w_raw[:, :, share:N].rearrange("p t m -> p m t"))
 
         nc.scalar.activation(along_x[:, 0, :], along_x[:, 1, :], COPY, bias=1.0, scale=-1.0)
 

@@ -56,9 +56,7 @@ def tile_picked_bilin_none_p_kernel(tc, x_words, x_scales, w1, fx, fy, offs, c00
         nc.sync.dma_start(l00[:], c00)
 
         w_bf = keep.tile([P, N, 4], BF16, align_bytes=64)
-        share = 80
-        nc.scalar.copy(w_bf[:, 0:share, :], w_raw[:, :, 0:share].rearrange("p t m -> p m t"))
-        nc.gpsimd.tensor_copy(w_bf[:, share:N, :], w_raw[:, :, share:N].rearrange("p t m -> p m t"))
+        nc.scalar.copy(w_bf[:], w_raw[:].rearrange("p t m -> p m t"))
 
         nc.scalar.activation(along_x[:, 0, :], along_x[:, 1, :], COPY, bias=1.0, scale=-1.0)
 

@@ -25,13 +25,13 @@ def tile_picked_bilin_none_p_kernel(tc, x_words, x_scales, w1, fx, fy, offs, c00
         reuse = ctx.enter_context(tc.tile_pool(name="reuse", bufs=1))
         psum = ctx.enter_context(tc.psum_pool(name="psum", bufs=1))
 
-        scale_win = keep.tile([P, T], U8, align_bytes=64)
+        scale_win = keep.tile([P, T], U8, align_bytes=256)
         nc.vector.memset(scale_win[:].bitcast(I32), 0)
         offs_sb = keep.tile([P, S // 16], U16)
-        word_win = keep.tile([P, T], U32, align_bytes=64)
-        w_raw = reuse.tile([P, 4, N], F32, align_bytes=64, offset=3072)
-        along_x = keep.tile([P, 2, V], F32, align_bytes=64)
-        fy_sb = keep.tile([P, V], F32, align_bytes=64)
+        word_win = keep.tile([P, T], U32, align_bytes=256)
+        w_raw = reuse.tile([P, 4, N], F32, align_bytes=256, offset=3072)
+        along_x = keep.tile([P, 2, V], F32, align_bytes=256)
+        fy_sb = keep.tile([P, V], F32, align_bytes=256)
         l11 = keep.tile([P, V // 16], U16)
         l10 = keep.tile([P, V // 16], U16)
         l01 = keep.tile([P, V // 16], U16)
@@ -103,7 +103,7 @@ def tile_picked_bilin_none_p_kernel(tc, x_words, x_scales, w1, fx, fy, offs, c00
         g00a = keep.tile([P, cut], F32)
         s1 = keep.tile([P, V], F32)
         s2 = keep.tile([P, V], F32)
-        res = keep.tile([P, V], F32)
+        res = keep.tile([P, V], F32, align_bytes=256)
         nc.vector.tensor_tensor(g11[:], y[:].indirect(l11[:]), w11, ALU.mult)
         nc.vector.tensor_tensor(g10[:], y[:].indirect(l10[:]), n10, ALU.mult)
         nc.vector.tensor_tensor(g01[:], y[:].indirect(l01[:]), n01, ALU.mult)

@@ -45,18 +45,20 @@ def tile_picked_bilin_none_p_kernel(tc, x_words, x_scales, w1, fx, fy, offs, c00
         nc.sync.dma_start(offs_sb[:], offs)
         load_scales(nc.sync, 0)
         load_scales(nc.sync, 1)
-        load_scales(nc.sync, 2)
+        load_scales(nc.scalar, 2)
         load_scales(nc.scalar, 3)
+        nc.sync.dma_start(l11[:], c11)
         nc.sync.dma_start(word_win[:].bitcast(I32), x_words[0].rearrange("p c r -> p (c r)").bitcast(I32))
         nc.sync.dma_start(along_x[:, 1, :], fx)
-        nc.sync.dma_start(l11[:], c11)
         nc.sync.dma_start(l10[:], c10)
         nc.sync.dma_start(fy_sb[:], fy)
         nc.sync.dma_start(l01[:], c01)
         nc.sync.dma_start(l00[:], c00)
 
         w_bf = keep.tile([P, N, 4], BF16, align_bytes=64)
-        nc.scalar.copy(w_bf[:], w_raw[:].rearrange("p t m -> p m t"))
+        share = 96
+        nc.scalar.copy(w_bf[:, 0:share, :], w_raw[:, :, 0:share].rearrange("p t m -> p m t"))
+        nc.gpsimd.tensor_copy(w_bf[:, share:N, :], w_raw[:, :, share:N].rearrange("p t m -> p m t"))
 
         nc.scalar.activation(along_x[:, 0, :], along_x[:, 1, :], COPY, bias=1.0, scale=-1.0)
 

@@ -56,9 +56,7 @@ def tile_picked_bilin_none_p_kernel(tc, x_words, x_scales, w1, fx, fy, offs, c00
         nc.sync.dma_start(l00[:], c00)
 
         w_bf = keep.tile([P, N, 4], BF16, align_bytes=64)
-        share = 96
-        nc.scalar.copy(w_bf[:, 0:share, :], w_raw[:, :, 0:share].rearrange("p t m -> p m t"))
-        nc.gpsimd.tensor_copy(w_bf[:, share:N, :], w_raw[:, :, share:N].rearrange("p t m -> p m t"))
+        nc.scalar.copy(w_bf[:], w_raw[:].rearrange("p t m -> p m t"))
 
         nc.scalar.activation(along_x[:, 0, :], along_x[:, 1, :], COPY, bias=1.0, scale=-1.0)
 
@@ -101,7 +99,7 @@ def tile_picked_bilin_none_p_kernel(tc, x_words, x_scales, w1, fx, fy, offs, c00
         g11 = keep.tile([P, V], F32)
         g10 = reuse.tile([P, V], F32, align_bytes=64, offset=6144)
         g01 = keep.tile([P, V], F32)
-        cut = 160
+        cut = 192
         g00a = keep.tile([P, cut], F32)
         s1 = keep.tile([P, V], F32)
         s2 = keep.tile([P, V], F32)

@@ -22,14 +22,13 @@ def tile_picked_bilin_none_p_kernel(tc, x_words, x_scales, w1, fx, fy, offs, c00
     nc = tc.nc
     with ExitStack() as ctx:
         keep = ctx.enter_context(tc.tile_pool(name="keep", bufs=1))
-        reuse = ctx.enter_context(tc.tile_pool(name="reuse", bufs=1))
         psum = ctx.enter_context(tc.psum_pool(name="psum", bufs=1))
 
         scale_win = keep.tile([P, T], U8, align_bytes=256)
-        nc.vector.memset(scale_win[:].bitcast(I32), 0)
+        nc.gpsimd.memset(scale_win[:].bitcast(I32), 0)
         offs_sb = keep.tile([P, S // 16], U16)
         word_win = keep.tile([P, T], U32, align_bytes=256)
-        w_raw = reuse.tile([P, 4, N], F32, align_bytes=256, offset=3072)
+        w_raw = keep.tile([P, 4, N], F32, align_bytes=256)
         along_x = keep.tile([P, 2, V], F32, align_bytes=256)
         fy_sb = keep.tile([P, V], F32, align_bytes=256)
         l11 = keep.tile([P, V // 16], U16)
@@ -82,7 +81,7 @@ def tile_picked_bilin_none_p_kernel(tc, x_words, x_scales, w1, fx, fy, offs, c00
 
         gather_scales(0, 512)
         quantize()
-        xa = reuse.tile([P, S], U32, align_bytes=64, offset=4096)
+        xa = keep.tile([P, S], U32, align_bytes=64)
         gather_words(xa, 0, 0, 256)
         project(xa, 0, 0, 256)
         gather_words(xa, 0, 256, 384)
@@ -90,28 +89,27 @@ def tile_picked_bilin_none_p_kernel(tc, x_words, x_scales, w1, fx, fy, offs, c00
         gather_words(xa, 0, 384, 512)
         project(xa, 0, 384, 512)
 
-        wts = reuse.tile([P, 2, 2, V], F32, align_bytes=64, offset=0)
+        wts = keep.tile([P, 2, 2, V], F32, align_bytes=64)
         fy_twice = fy_sb[:].unsqueeze(1).to_broadcast([P, 2, V])
         nc.vector.tensor_tensor(wts[:, 1, :, :], fy_twice, along_x[:], ALU.mult)
         nc.vector.scalar_tensor_tensor(wts[:, 0, :, :], fy_twice, 1.0, along_x[:], ALU.subtract, ALU.mult)
         w11, n10, n01, n00 = wts[:, 1, 1, :], wts[:, 1, 0, :], wts[:, 0, 1, :], wts[:, 0, 0, :]
 
         g11 = keep.tile([P, V], F32)
-        g10 = reuse.tile([P, V], F32, align_bytes=64, offset=6144)
+        g10 = keep.tile([P, V], F32)
         g01 = keep.tile([P, V], F32)
-        cut = 192
-        g00a = keep.tile([P, cut], F32)
+        g00 = keep.tile([P, V], F32)
         s1 = keep.tile([P, V], F32)
-        s2 = keep.tile([P, V], F32)
         res = keep.tile([P, V], F32, align_bytes=256)
         nc.vector.tensor_tensor(g11[:], y[:].indirect(l11[:]), w11, ALU.mult)
         nc.vector.tensor_tensor(g10[:], y[:].indirect(l10[:]), n10, ALU.mult)
         nc.vector.tensor_tensor(g01[:], y[:].indirect(l01[:]), n01, ALU.mult)
         nc.vector.tensor_tensor(s1[:], g11[:], g10[:], ALU.add)
-        nc.vector.tensor_tensor(g00a[:], y[:].indirect(l00[:, 0 : cut // 16]), n00[:, 0:cut], ALU.mult)
-        nc.vector.tensor_tensor(s2[:], s1[:], g01[:], ALU.subtract)
-        g00b = reuse.tile([P, V - cut], F32, align_bytes=64, offset=6144)
-        nc.vector.tensor_tensor(g00b[:], y[:].indirect(l00[:, cut // 16 : V // 16]), n00[:, cut:V], ALU.mult)
-        nc.vector.tensor_tensor(res[:, 0:cut], s2[:, 0:cut], g00a[:], ALU.subtract)
-        nc.vector.tensor_tensor(res[:, cut:V], s2[:, cut:V], g00b[:], ALU.subtract)
+        nc.vector.tensor_tensor(g00[:], y[:].indirect(l00[:]), n00, ALU.mult)
+        s2 = keep.tile([P, V], F32)
+        parts = [slice(0, 88), slice(88, 176), slice(176, 256)]
+        for part in parts:
+            nc.vector.tensor_tensor(s2[:, part], s1[:, part], g01[:, part], ALU.subtract)
+        for part in parts:
+            nc.vector.tensor_tensor(res[:, part], s2[:, part], g00[:, part], ALU.subtract)
         nc.sync.dma_start(out, res[:])

@@ -44,13 +44,13 @@ def tile_picked_bilin_none_p_kernel(tc, x_words, x_scales, w1, fx, fy, offs, c00
         nc.sync.dma_start(offs_sb[:], offs)
         load_scales(nc.sync, 0)
         load_scales(nc.sync, 1)
-        load_scales(nc.scalar, 2)
+        load_scales(nc.sync, 2)
         load_scales(nc.scalar, 3)
-        nc.sync.dma_start(l11[:], c11)
         nc.sync.dma_start(word_win[:].bitcast(I32), x_words[0].rearrange("p c r -> p (c r)").bitcast(I32))
         nc.sync.dma_start(along_x[:, 1, :], fx)
-        nc.sync.dma_start(l10[:], c10)
+        nc.sync.dma_start(l11[:], c11)
         nc.sync.dma_start(fy_sb[:], fy)
+        nc.sync.dma_start(l10[:], c10)
         nc.sync.dma_start(l01[:], c01)
         nc.sync.dma_start(l00[:], c00)
 

@@ -26,9 +26,10 @@ def tile_picked_bilin_none_p_kernel(tc, x_words, x_scales, w1, fx, fy, offs, c00
 
         scale_win = keep.tile([P, T], U8, align_bytes=256)
         nc.gpsimd.memset(scale_win[:].bitcast(I32), 0)
+
+        w_raw = keep.tile([P, 4, N], F32, align_bytes=256)
         offs_sb = keep.tile([P, S // 16], U16)
         word_win = keep.tile([P, T], U32, align_bytes=256)
-        w_raw = keep.tile([P, 4, N], F32, align_bytes=256)
         along_x = keep.tile([P, 2, V], F32, align_bytes=256)
         fy_sb = keep.tile([P, V], F32, align_bytes=256)
         l11 = keep.tile([P, V // 16], U16)
@@ -36,23 +37,18 @@ def tile_picked_bilin_none_p_kernel(tc, x_words, x_scales, w1, fx, fy, offs, c00
         l01 = keep.tile([P, V // 16], U16)
         l00 = keep.tile([P, V // 16], U16)
 
-        def load_scales(eng, q):
-            eng.dma_start(scale_win[q:P:32, :].bitcast(I32), x_scales[0].rearrange("(a r) c -> r a c", r=4)[q].bitcast(I32))
-
-        w_rows = w1.rearrange("(p j) m -> p j m", j=4)
-        nc.sync.dma_start(w_raw[:], w_rows)
+        scale_rows = x_scales[0].rearrange("(a r) c -> r a c", r=4)
+        nc.sync.dma_start(w_raw[:], w1.rearrange("(p j) m -> p j m", j=4))
         nc.sync.dma_start(offs_sb[:], offs)
-        load_scales(nc.sync, 0)
-        load_scales(nc.sync, 1)
-        load_scales(nc.sync, 2)
-        load_scales(nc.scalar, 3)
+        for r, queue in enumerate((nc.sync, nc.sync, nc.sync, nc.scalar)):
+            queue.dma_start(scale_win[r:P:32, :].bitcast(I32), scale_rows[r].bitcast(I32))
         nc.sync.dma_start(word_win[:].bitcast(I32), x_words[0].rearrange("p c r -> p (c r)").bitcast(I32))
         nc.sync.dma_start(along_x[:, 1, :], fx)
-        nc.sync.dma_start(l11[:], c11)
-        nc.sync.dma_start(fy_sb[:], fy)
-        nc.sync.dma_start(l10[:], c10)
         nc.sync.dma_start(l01[:], c01)
         nc.sync.dma_start(l00[:], c00)
+        nc.sync.dma_start(l11[:], c11)
+        nc.sync.dma_start(l10[:], c10)
+        nc.sync.dma_start(fy_sb[:], fy)
 
         w_bf = keep.tile([P, N, 4], BF16, align_bytes=64)
         nc.scalar.copy(w_bf[:], w_raw[:].rearrange("p t m -> p m t"))
@@ -60,56 +56,45 @@ def tile_picked_bilin_none_p_kernel(tc, x_words, x_scales, w1, fx, fy, offs, c00
         nc.scalar.activation(along_x[:, 0, :], along_x[:, 1, :], COPY, bias=1.0, scale=-1.0)
 
         x_sc = keep.tile([P, S], U8, align_bytes=64)
+        x_codes = keep.tile([P, S], U32, align_bytes=64)
         w_codes = keep.tile([P, N], U32, align_bytes=64)
         w_sc = keep.tile([P, N], U8, align_bytes=64)
         y = keep.tile([P, S], F32, align_bytes=64)
 
-        def gather_scales(a, b):
-            nc.vector.tensor_copy(x_sc[:, a:b], scale_win[:].indirect(offs_sb[:, a // 16 : b // 16]))
-
-        def gather_words(xc, o, a, b):
-            nc.vector.tensor_copy(xc[:, a - o : b - o], word_win[:].indirect(offs_sb[:, a // 16 : b // 16]))
-
-        def quantize():
-            nc.vector.quantize_mx(out=w_codes[:].bitcast(FP8X4), scales=w_sc[:], in_=w_bf[:].rearrange("p m t -> p (m t)"))
-
-        def project(xc, o, a, b):
+        nc.vector.tensor_copy(x_sc[:], scale_win[:].indirect(offs_sb[:]))
+        nc.vector.quantize_mx(out=w_codes[:].bitcast(FP8X4), scales=w_sc[:], in_=w_bf[:].rearrange("p m t -> p (m t)"))
+        for a, b in ((0, 256), (256, 384), (384, 512)):
+            nc.vector.tensor_copy(x_codes[:, a:b], word_win[:].indirect(offs_sb[:, a // 16 : b // 16]))
             acc = psum.tile([P, 512], F32, name="acc%d" % a)
             nc.tensor.matmul_mx(out=acc[:, 0 : b - a], lhsT=w_codes[:].bitcast(FP8X4), lhsT_scale=w_sc[:],
-                                rhs=xc[:, a - o : b - o].bitcast(FP8X4), rhs_scale=x_sc[:, a:b], start=True, stop=True)
+                                rhs=x_codes[:, a:b].bitcast(FP8X4), rhs_scale=x_sc[:, a:b], start=True, stop=True)
             nc.scalar.copy(y[:, a:b], acc[:, 0 : b - a])
-
-        gather_scales(0, 512)
-        quantize()
-        xa = keep.tile([P, S], U32, align_bytes=64)
-        gather_words(xa, 0, 0, 256)
-        project(xa, 0, 0, 256)
-        gather_words(xa, 0, 256, 384)
-        project(xa, 0, 256, 384)
-        gather_words(xa, 0, 384, 512)
-        project(xa, 0, 384, 512)
 
         wts = keep.tile([P, 2, 2, V], F32, align_bytes=64)
         fy_twice = fy_sb[:].unsqueeze(1).to_broadcast([P, 2, V])
         nc.vector.tensor_tensor(wts[:, 1, :, :], fy_twice, along_x[:], ALU.mult)
         nc.vector.scalar_tensor_tensor(wts[:, 0, :, :], fy_twice, 1.0, along_x[:], ALU.subtract, ALU.mult)
-        w11, n10, n01, n00 = wts[:, 1, 1, :], wts[:, 1, 0, :], wts[:, 0, 1, :], wts[:, 0, 0, :]
 
-        g11 = keep.tile([P, V], F32)
-        g10 = keep.tile([P, V], F32)
+        p11 = keep.tile([P, V], F32)
+        p10 = keep.tile([P, V], F32)
         g01 = keep.tile([P, V], F32)
         g00 = keep.tile([P, V], F32)
-        s1 = keep.tile([P, V], F32)
+        p01 = keep.tile([P, V], F32)
+        p00 = keep.tile([P, V], F32)
+        low = keep.tile([P, V], F32)
+        three = keep.tile([P, V], F32)
         res = keep.tile([P, V], F32, align_bytes=256)
-        nc.vector.tensor_tensor(g11[:], y[:].indirect(l11[:]), w11, ALU.mult)
-        nc.vector.tensor_tensor(g10[:], y[:].indirect(l10[:]), n10, ALU.mult)
-        nc.vector.tensor_tensor(g01[:], y[:].indirect(l01[:]), n01, ALU.mult)
-        nc.vector.tensor_tensor(s1[:], g11[:], g10[:], ALU.add)
-        nc.vector.tensor_tensor(g00[:], y[:].indirect(l00[:]), n00, ALU.mult)
-        s2 = keep.tile([P, V], F32)
+        nc.scalar.activation(g01[:], y[:].indirect(l01[:]), COPY)
+        nc.scalar.activation(g00[:], y[:].indirect(l00[:]), COPY)
+        nc.vector.tensor_tensor(p11[:], y[:].indirect(l11[:]), wts[:, 1, 1, :], ALU.mult)
+        nc.vector.tensor_tensor(p10[:], y[:].indirect(l10[:]), wts[:, 1, 0, :], ALU.mult)
+
+        nc.vector.tensor_tensor(p01[:], g01[:], wts[:, 0, 1, :], ALU.mult)
+        nc.vector.tensor_tensor(low[:], p11[:], p10[:], ALU.add)
+        nc.vector.tensor_tensor(p00[:], g00[:], wts[:, 0, 0, :], ALU.mult)
         parts = [slice(0, 88), slice(88, 176), slice(176, 256)]
         for part in parts:
-            nc.vector.tensor_tensor(s2[:, part], s1[:, part], g01[:, part], ALU.subtract)
+            nc.vector.tensor_tensor(three[:, part], low[:, part], p01[:, part], ALU.subtract)
         for part in parts:
-            nc.vector.tensor_tensor(res[:, part], s2[:, part], g00[:, part], ALU.subtract)
+            nc.vector.tensor_tensor(res[:, part], three[:, part], p00[:, part], ALU.subtract)
         nc.sync.dma_start(out, res[:])

@@ -44,10 +44,10 @@ def tile_picked_bilin_none_p_kernel(tc, x_words, x_scales, w1, fx, fy, offs, c00
             queue.dma_start(scale_win[r:P:32, :].bitcast(I32), scale_rows[r].bitcast(I32))
         nc.sync.dma_start(word_win[:].bitcast(I32), x_words[0].rearrange("p c r -> p (c r)").bitcast(I32))
         nc.sync.dma_start(along_x[:, 1, :], fx)
+        nc.sync.dma_start(l10[:], c10)
         nc.sync.dma_start(l01[:], c01)
         nc.sync.dma_start(l00[:], c00)
         nc.sync.dma_start(l11[:], c11)
-        nc.sync.dma_start(l10[:], c10)
         nc.sync.dma_start(fy_sb[:], fy)
 
         w_bf = keep.tile([P, N, 4], BF16, align_bytes=64)
@@ -63,7 +63,7 @@ def tile_picked_bilin_none_p_kernel(tc, x_words, x_scales, w1, fx, fy, offs, c00
 
         nc.vector.tensor_copy(x_sc[:], scale_win[:].indirect(offs_sb[:]))
         nc.vector.quantize_mx(out=w_codes[:].bitcast(FP8X4), scales=w_sc[:], in_=w_bf[:].rearrange("p m t -> p (m t)"))
-        for a, b in ((0, 256), (256, 384), (384, 512)):
+        for a, b in ((0, 256), (256, 384), (384, 448), (448, 512)):
             nc.vector.tensor_copy(x_codes[:, a:b], word_win[:].indirect(offs_sb[:, a // 16 : b // 16]))
             acc = psum.tile([P, 512], F32, name="acc%d" % a)
             nc.tensor.matmul_mx(out=acc[:, 0 : b - a], lhsT=w_codes[:].bitcast(FP8X4), lhsT_scale=w_sc[:],
@@ -75,20 +75,24 @@ def tile_picked_bilin_none_p_kernel(tc, x_words, x_scales, w1, fx, fy, offs, c00
         nc.vector.tensor_tensor(wts[:, 1, :, :], fy_twice, along_x[:], ALU.mult)
         nc.vector.scalar_tensor_tensor(wts[:, 0, :, :], fy_twice, 1.0, along_x[:], ALU.subtract, ALU.mult)
 
+        cut = 64
+        first, rest = slice(0, cut), slice(cut, V)
         p11 = keep.tile([P, V], F32)
         p10 = keep.tile([P, V], F32)
         g01 = keep.tile([P, V], F32)
         g00 = keep.tile([P, V], F32)
+        g10 = keep.tile([P, cut], F32)
         p01 = keep.tile([P, V], F32)
         p00 = keep.tile([P, V], F32)
         low = keep.tile([P, V], F32)
         three = keep.tile([P, V], F32)
         res = keep.tile([P, V], F32, align_bytes=256)
+        nc.scalar.activation(g10[:], y[:].indirect(l10[:, 0 : cut // 16]), COPY)
         nc.scalar.activation(g01[:], y[:].indirect(l01[:]), COPY)
         nc.scalar.activation(g00[:], y[:].indirect(l00[:]), COPY)
         nc.vector.tensor_tensor(p11[:], y[:].indirect(l11[:]), wts[:, 1, 1, :], ALU.mult)
-        nc.vector.tensor_tensor(p10[:], y[:].indirect(l10[:]), wts[:, 1, 0, :], ALU.mult)
-
+        nc.vector.tensor_tensor(p10[:, rest], y[:].indirect(l10[:, cut // 16 : V // 16]), wts[:, 1, 0, rest], ALU.mult)
+        nc.vector.tensor_tensor(p10[:, first], g10[:], wts[:, 1, 0, first], ALU.mult)
         nc.vector.tensor_tensor(p01[:], g01[:], wts[:, 0, 1, :], ALU.mult)
         nc.vector.tensor_tensor(low[:], p11[:], p10[:], ALU.add)
         nc.vector.tensor_tensor(p00[:], g00[:], wts[:, 0, 0, :], ALU.mult)

@@ -45,10 +45,10 @@ def tile_picked_bilin_none_p_kernel(tc, x_words, x_scales, w1, fx, fy, offs, c00
         nc.sync.dma_start(word_win[:].bitcast(I32), x_words[0].rearrange("p c r -> p (c r)").bitcast(I32))
         nc.sync.dma_start(along_x[:, 1, :], fx)
         nc.sync.dma_start(l10[:], c10)
+        nc.sync.dma_start(fy_sb[:], fy)
+        nc.sync.dma_start(l11[:], c11)
         nc.sync.dma_start(l01[:], c01)
         nc.sync.dma_start(l00[:], c00)
-        nc.sync.dma_start(l11[:], c11)
-        nc.sync.dma_start(fy_sb[:], fy)
 
         w_bf = keep.tile([P, N, 4], BF16, align_bytes=64)
         nc.scalar.copy(w_bf[:], w_raw[:].rearrange("p t m -> p m t"))

@@ -38,8 +38,8 @@ def tile_picked_bilin_none_p_kernel(tc, x_words, x_scales, w1, fx, fy, offs, c00
         l00 = keep.tile([P, V // 16], U16)
 
         scale_rows = x_scales[0].rearrange("(a r) c -> r a c", r=4)
-        nc.sync.dma_start(w_raw[:], w1.rearrange("(p j) m -> p j m", j=4))
         nc.sync.dma_start(offs_sb[:], offs)
+        nc.sync.dma_start(w_raw[:], w1.rearrange("(p j) m -> p j m", j=4))
         for r, queue in enumerate((nc.sync, nc.sync, nc.sync, nc.scalar)):
             queue.dma_start(scale_win[r:P:32, :].bitcast(I32), scale_rows[r].bitcast(I32))
         nc.sync.dma_start(word_win[:].bitcast(I32), x_words[0].rearrange("p c r -> p (c r)").bitcast(I32))

from contextlib import ExitStack

import concourse.mybir as mybir

K, T, S, V, N = 512, 1024, 512, 256, 128
FLOPS = 2 * K * S * N

F32 = mybir.dt.float32
BF16 = mybir.dt.bfloat16
I32 = mybir.dt.int32
U32 = mybir.dt.uint32
U16 = mybir.dt.uint16
U8 = mybir.dt.uint8
FP8X4 = mybir.dt.float8_e4m3fn_x4
ALU = mybir.AluOpType
COPY = mybir.ActivationFunctionType.Copy

P = 128


def tile_picked_bilin_none_p_kernel(tc, x_words, x_scales, w1, fx, fy, offs, c00, c01, c10, c11, out):
    nc = tc.nc
    with ExitStack() as ctx:
        keep = ctx.enter_context(tc.tile_pool(name="keep", bufs=1))
        psum = ctx.enter_context(tc.psum_pool(name="psum", bufs=1))

        scale_win = keep.tile([P, T], U8, align_bytes=256)
        nc.gpsimd.memset(scale_win[:].bitcast(I32), 0)

        w_raw = keep.tile([P, 4, N], F32, align_bytes=256)
        offs_sb = keep.tile([P, S // 16], U16)
        word_win = keep.tile([P, T], U32, align_bytes=256)
        along_x = keep.tile([P, 2, V], F32, align_bytes=256)
        fy_sb = keep.tile([P, V], F32, align_bytes=256)
        l11 = keep.tile([P, V // 16], U16)
        l10 = keep.tile([P, V // 16], U16)
        l01 = keep.tile([P, V // 16], U16)
        l00 = keep.tile([P, V // 16], U16)

        scale_rows = x_scales[0].rearrange("(a r) c -> r a c", r=4)
        nc.sync.dma_start(offs_sb[:], offs)
        nc.sync.dma_start(w_raw[:], w1.rearrange("(p j) m -> p j m", j=4))
        for r, queue in enumerate((nc.sync, nc.sync, nc.sync, nc.scalar)):
            queue.dma_start(scale_win[r:P:32, :].bitcast(I32), scale_rows[r].bitcast(I32))
        nc.sync.dma_start(word_win[:].bitcast(I32), x_words[0].rearrange("p c r -> p (c r)").bitcast(I32))
        nc.sync.dma_start(along_x[:, 1, :], fx)
        nc.sync.dma_start(l10[:], c10)
        nc.sync.dma_start(fy_sb[:], fy)
        nc.sync.dma_start(l11[:], c11)
        nc.sync.dma_start(l01[:], c01)
        nc.sync.dma_start(l00[:], c00)

        w_bf = keep.tile([P, N, 4], BF16, align_bytes=64)
        nc.scalar.copy(w_bf[:], w_raw[:].rearrange("p t m -> p m t"))

        nc.scalar.activation(along_x[:, 0, :], along_x[:, 1, :], COPY, bias=1.0, scale=-1.0)

        x_sc = keep.tile([P, S], U8, align_bytes=64)
        x_codes = keep.tile([P, S], U32, align_bytes=64)
        w_codes = keep.tile([P, N], U32, align_bytes=64)
        w_sc = keep.tile([P, N], U8, align_bytes=64)
        y = keep.tile([P, S], F32, align_bytes=64)

        nc.vector.tensor_copy(x_sc[:], scale_win[:].indirect(offs_sb[:]))
        nc.vector.quantize_mx(out=w_codes[:].bitcast(FP8X4), scales=w_sc[:], in_=w_bf[:].rearrange("p m t -> p (m t)"))
        for a, b in ((0, 256), (256, 384), (384, 448), (448, 512)):
            nc.vector.tensor_copy(x_codes[:, a:b], word_win[:].indirect(offs_sb[:, a // 16 : b // 16]))
            acc = psum.tile([P, 512], F32, name="acc%d" % a)
            nc.tensor.matmul_mx(out=acc[:, 0 : b - a], lhsT=w_codes[:].bitcast(FP8X4), lhsT_scale=w_sc[:],
                                rhs=x_codes[:, a:b].bitcast(FP8X4), rhs_scale=x_sc[:, a:b], start=True, stop=True)
            nc.scalar.copy(y[:, a:b], acc[:, 0 : b - a])

        wts = keep.tile([P, 2, 2, V], F32, align_bytes=64)
        fy_twice = fy_sb[:].unsqueeze(1).to_broadcast([P, 2, V])
        nc.vector.tensor_tensor(wts[:, 1, :, :], fy_twice, along_x[:], ALU.mult)
        nc.vector.scalar_tensor_tensor(wts[:, 0, :, :], fy_twice, 1.0, along_x[:], ALU.subtract, ALU.mult)

        cut = 64
        first, rest = slice(0, cut), slice(cut, V)
        p11 = keep.tile([P, V], F32)
        p10 = keep.tile([P, V], F32)
        g01 = keep.tile([P, V], F32)
        g00 = keep.tile([P, V], F32)
        g10 = keep.tile([P, cut], F32)
        p01 = keep.tile([P, V], F32)
        p00 = keep.tile([P, V], F32)
        low = keep.tile([P, V], F32)
        three = keep.tile([P, V], F32)
        res = keep.tile([P, V], F32, align_bytes=256)
        nc.scalar.activation(g10[:], y[:].indirect(l10[:, 0 : cut // 16]), COPY)
        nc.scalar.activation(g01[:], y[:].indirect(l01[:]), COPY)
        nc.scalar.activation(g00[:], y[:].indirect(l00[:]), COPY)
        nc.vector.tensor_tensor(p11[:], y[:].indirect(l11[:]), wts[:, 1, 1, :], ALU.mult)
        nc.vector.tensor_tensor(p10[:, rest], y[:].indirect(l10[:, cut // 16 : V // 16]), wts[:, 1, 0, rest], ALU.mult)
        nc.vector.tensor_tensor(p10[:, first], g10[:], wts[:, 1, 0, first], ALU.mult)
        nc.vector.tensor_tensor(p01[:], g01[:], wts[:, 0, 1, :], ALU.mult)
        nc.vector.tensor_tensor(low[:], p11[:], p10[:], ALU.add)
        nc.vector.tensor_tensor(p00[:], g00[:], wts[:, 0, 0, :], ALU.mult)
        parts = [slice(0, 88), slice(88, 176), slice(176, 256)]
        for part in parts:
            nc.vector.tensor_tensor(three[:, part], low[:, part], p01[:, part], ALU.subtract)
        for part in parts:
            nc.vector.tensor_tensor(res[:, part], three[:, part], p00[:, part], ALU.subtract)
        nc.sync.dma_start(out, res[:])
